import numpy as np
import ml_dtypes


def mxq(x, axis, fmt="e4m3"):
    dtype, down = {"e4m3": (ml_dtypes.float8_e4m3fn, 7), "e5m2": (ml_dtypes.float8_e5m2, 14)}[fmt]
    v = np.moveaxis(np.asarray(x, np.float32).astype(ml_dtypes.bfloat16).astype(np.float64), axis, -1)
    blocks = v.reshape(v.shape[:-1] + (-1, 32))
    amax = np.abs(blocks).max(-1, keepdims=True)
    byte = np.maximum(np.where(amax > 0, np.frexp(amax)[1] - 1 + 127, 0) - down, 1)
    scale = np.exp2(byte - 127.0)
    codes = (blocks / scale).astype(np.float32).astype(dtype).astype(np.float64)
    return np.moveaxis((codes * scale).reshape(v.shape), -1, axis)


WIDE = False


def mx_kscale(k):
    if not WIDE:
        return np.ones(k)
    levels = np.array([10, -10, 5, -5, 0])
    if k % 512:
        return np.exp2(np.random.permutation(np.resize(levels, k // 32))).repeat(32)
    a = np.empty((k // 512, 16))
    for p in range(k // 512):
        a[p, :8] = np.random.permutation(np.resize(levels, 8))
        for g in range(8):
            far = levels[np.abs(levels - a[p, g]) >= 10]
            a[p, g + 8] = far[np.random.randint(len(far))]
    return np.exp2(a.ravel()).repeat(32)


def f64(x):
    return np.asarray(x).astype(np.float64)


def striped(idx):
    return np.tile(idx.reshape(-1, 16).T, (8, 1)).astype(np.uint16)


def unstriped(offs):
    return offs[:16].T.reshape(-1).astype(np.int64)


def striped8(idx):
    return np.concatenate([x.reshape(-1, 16).T for x in idx]).astype(np.uint16)


def runs(offs, k):
    lists = np.stack([offs[16 * r : 16 * r + 16].T.reshape(-1) for r in range(8)]).astype(np.int64)
    return lists[np.arange(k) % 512 // 64]


def pack_weight(w):
    k, n = w.shape
    w = f64(np.asarray(w, np.float32).astype(ml_dtypes.bfloat16)).reshape(k // 32, 32, n)
    amax = np.abs(w).max(1)
    byte = np.clip(np.where(amax > 0, np.frexp(amax)[1] - 1 + 127 - 7, 1), 1, 254)
    scaled = (w * np.exp2(127.0 - byte)[:, None, :]).reshape(k, n).astype(np.float32)
    words = np.ascontiguousarray(scaled.reshape(k // 512, 128, 4, n).transpose(0, 1, 3, 2)).astype(ml_dtypes.float8_e4m3fn).view(np.uint8)
    return words, np.ascontiguousarray(byte.astype(np.uint8).reshape(k // 512, 16, n))


def unpack_weight(words, scales):
    g, p, n, _ = words.shape
    vals = np.ascontiguousarray(words).view(ml_dtypes.float8_e4m3fn).astype(np.float64) * np.repeat(np.exp2(scales.astype(np.float64) - 127.0), 8, axis=1)[..., None]
    return vals.transpose(0, 1, 3, 2).reshape(g * 512, n)


K, T, S, N, H = 512, 2048, 512, 512, 512


def setup_inputs():
    n = np.random.standard_normal
    s = mx_kscale(K)[:, None]
    u = mx_kscale(H)
    packed_xT = pack_weight(n((K, T)) * s)
    return {
        "x_words": packed_xT[0],
        "x_scales": packed_xT[1],
        "w1": (n((K, H)) / np.sqrt(K) / s).astype(np.float32),
        "gn": (np.random.uniform(0.5, 1.5, (H, 1)) * u[:, None]).astype(np.float32),
        "w2": (n((H, N)) / np.sqrt(H) / u[:, None]).astype(np.float32),
        "w3": (n((K, N)) / np.sqrt(K) / s).astype(np.float32),
        "offs": striped(np.random.permutation(T)[:S]),
        "n1": striped8(np.stack([np.random.permutation(S) for _ in range(8)])),
        "two": striped(np.random.permutation(T)[:S]),
        "n2": striped8(np.stack([np.random.permutation(S) for _ in range(8)])),
        "n3": striped8(np.stack([np.random.permutation(S) for _ in range(8)])),
    }


def reference(x_words, x_scales, w1, gn, w2, w3, offs, n1, two, n2, n3):
    xq = unpack_weight(x_words, x_scales)[:, unstriped(offs)]
    y = mxq(f64(w1), 0, "e4m3").T @ xq
    z = f64(gn) * (np.maximum(y, y[np.arange(H)[:, None], runs(n1, H)]))
    h = mxq(f64(w2), 0, "e4m3").T @ mxq(z, 0, "e4m3")
    x_two = unpack_weight(x_words, x_scales)[:, unstriped(two)]
    d = mxq(f64(w3), 0, "e4m3").T @ x_two
    return 0.75 * (h * (d[np.arange(N)[:, None], runs(n3, N)]) - ((h[np.arange(N)[:, None], runs(n2, N)]) * d))

@@ -1,0 +1,230 @@
+from contextlib import ExitStack
+
+import concourse.mybir as mybir
+from concourse.masks import make_identity
+
+K, T, S, N, H = 512, 2048, 512, 512, 512
+FLOPS = 3 * 2 * 512 * 512 * 512
+
+F32 = mybir.dt.float32
+BF16 = mybir.dt.bfloat16
+I32 = mybir.dt.int32
+U32 = mybir.dt.uint32
+U16 = mybir.dt.uint16
+U8 = mybir.dt.uint8
+FP8X4 = mybir.dt.float8_e4m3fn_x4
+ALU = mybir.AluOpType
+COPY = mybir.ActivationFunctionType.Copy
+
+P = 128
+PACK = 4
+HALF = S // 2
+LIST_COLS = S // 16
+
+
+def tile_picked_latecrossbbig_none_p_kernel(
+    tc, x_words, x_scales, w1, gn, w2, w3, offs, n1, two, n2, n3, out
+):
+    nc = tc.nc
+    with ExitStack() as ctx:
+        keep = ctx.enter_context(tc.tile_pool(name="keep", bufs=1))
+        psum = ctx.enter_context(tc.psum_pool(name="psum", bufs=1))
+
+        def load_list(name, src):
+            t = keep.tile([P, LIST_COLS], U16, name=name)
+            nc.sync.dma_start(t[:], src)
+            return t
+
+        def load_weight(name, src):
+            t = keep.tile([P, PACK, 512], F32, name=name)
+            nc.sync.dma_start(out=t[:], in_=src.rearrange("(p j) c -> p j c", j=PACK))
+            return t
+
+        def half_list(t, h):
+            return t[:, h * (LIST_COLS // 2) : (h + 1) * (LIST_COLS // 2)]
+
+        def cols(h):
+            return slice(h * HALF, (h + 1) * HALF)
+
+        x_bytes = keep.tile([P, T], U8, name="x_bytes", align_bytes=64)
+        nc.vector.memset(x_bytes[:].bitcast(I32), 0)
+        gain_block = keep.tile([P, 32], F32, name="gain_block")
+        nc.sync.dma_start(out=gain_block[:], in_=gn.rearrange("(b c) o -> b o c", c=32).to_broadcast([16, 8, 32]))
+        x_codes = keep.tile([P, T], U32, name="x_codes", align_bytes=64)
+        nc.sync.dma_start(out=x_codes[:].bitcast(I32), in_=x_words[0].rearrange("p n t -> p (n t)").bitcast(I32))
+        offs_t = load_list("offs_t", offs)
+        two_t = load_list("two_t", two)
+        n1_t = load_list("n1_t", n1)
+        n3_t = load_list("n3_t", n3)
+        n2_t = load_list("n2_t", n2)
+        w1_raw = load_weight("w1_raw", w1)
+        scale_rows = x_scales[0].bitcast(I32)
+        for q in range(4):
+            nc.sync.dma_start(out=x_bytes[32 * q : 32 * q + 4, :].bitcast(I32), in_=scale_rows[4 * q : 4 * q + 4, :])
+        w2_rows = w2.rearrange("(b j i) c -> j b i c", j=PACK, i=8)
+        w2_raw = [keep.tile([P, 512], F32, name="w2_raw%d" % j) for j in range(PACK)]
+        for j in range(PACK):
+            nc.sync.dma_start(out=w2_raw[j][:], in_=w2_rows[j])
+        w3_raw = load_weight("w3_raw", w3)
+
+        ident = keep.tile([P, P], F32, name="ident")
+        make_identity(nc, ident[:])
+        own = keep.tile([P, 8], F32, name="own")
+        nc.vector.tensor_reduce(own[:], ident[:].rearrange("p (b i) -> p i b", i=8), mybir.AxisListType.X, ALU.add)
+        picked = keep.tile([P, PACK, 8], F32, name="picked", align_bytes=64)
+        nc.vector.tensor_tensor(
+            picked[:], gain_block[:].rearrange("p (t i) -> p t i", i=8),
+            own[:].unsqueeze(1).to_broadcast([P, PACK, 8]), ALU.mult,
+        )
+        gain = keep.tile([P, PACK], F32, name="gain")
+        nc.vector.tensor_reduce(gain[:], picked[:], mybir.AxisListType.X, ALU.add)
+        mag = keep.tile([P, PACK], F32, name="mag")
+        nc.vector.tensor_reduce(mag[:], picked[:], mybir.AxisListType.X, ALU.add, apply_absolute_value=True)
+        nonneg = keep.tile([P, PACK], F32, name="nonneg", align_bytes=64)
+        nc.vector.tensor_scalar(nonneg[:], gain[:], 0.0, 2.0, ALU.is_ge, ALU.mult)
+        sign = keep.tile([P, PACK], F32, name="sign")
+        nc.vector.tensor_scalar(sign[:], nonneg[:], 1.0, -1.0, ALU.mult, ALU.add)
+
+        def gather_bytes(name, lst):
+            t = keep.tile([P, S], U8, name=name, align_bytes=64)
+            nc.vector.tensor_copy(t[:], x_bytes[:].indirect(lst[:]))
+            return t
+
+        def gather_words(name, lst):
+            t = keep.tile([P, S], U32, name=name, align_bytes=64)
+            nc.vector.tensor_copy(t[:], x_codes[:].indirect(lst[:]))
+            return t
+
+        def quantize(name, grouped, width):
+            codes = keep.tile([P, width], U32, name=name + "_codes", align_bytes=64)
+            scales = keep.tile([P, width], U8, name=name + "_scales", align_bytes=64)
+            nc.vector.quantize_mx(out=codes[:].bitcast(FP8X4), scales=scales[:], in_=grouped)
+            return codes, scales
+
+        def product(acc, w_q, t, codes, scales):
+            m = slice(t * P, (t + 1) * P)
+            nc.tensor.matmul_mx(
+                out=acc, lhsT=w_q[0][:, m].bitcast(FP8X4), lhsT_scale=w_q[1][:, m],
+                rhs=codes.bitcast(FP8X4), rhs_scale=scales, start=True, stop=True,
+            )
+
+        def deal(dst, src, t):
+            nc.scalar.copy(
+                out=dst.rearrange("p (b i j) -> p b j i", i=8, j=PACK),
+                in_=src[:].rearrange("p j (b t i) -> p t b j i", t=PACK, i=8)[:, t],
+            )
+
+        a_words = gather_words("nonneg", offs_t)
+        b_words = gather_words("picked", two_t)
+        a_bytes = gather_bytes("a_bytes", offs_t)
+        w1_q = []
+        for t in range(PACK):
+            w1_g = keep.tile([P, 512], BF16, name="w1_g%d" % t, align_bytes=64)
+            deal(w1_g[:], w1_raw, t)
+            w1_q.append(quantize("w1_%d" % t, w1_g[:], P))
+            if t == 1:
+                b_bytes = gather_bytes("w1_g1", two_t)
+
+        y = []
+        for t in range(PACK):
+            acc = psum.tile([P, S], F32, name="bank%d" % t)
+            product(acc[:], w1_q[t], 0, a_words[:], a_bytes[:])
+            y_t = keep.tile([P, S], F32, name="y%d" % t)
+            nc.scalar.activation(y_t[:], acc[:], COPY, scale=mag[:, t : t + 1])
+            y.append(y_t)
+
+        w2_signed = keep.tile([P, PACK, 512], BF16, name="mag")
+        for j in range(PACK):
+            nc.scalar.activation(w2_signed[:, j, :], w2_raw[j][:], COPY, scale=sign[:, j : j + 1])
+
+        w2_g = keep.tile([P, 512 * PACK], BF16, name="w2_g", align_bytes=64)
+        w3_g = keep.tile([P, 512 * PACK], BF16, name="w3_g", align_bytes=64)
+        for t in range(PACK):
+            deal(w2_g[:, 512 * t : 512 * (t + 1)], w2_signed, t)
+        for t in range(PACK):
+            deal(w3_g[:, 512 * t : 512 * (t + 1)], w3_raw, t)
+
+        fetched = [keep.tile([P, PACK, HALF], F32, name="fetched%d" % h) for h in range(2)]
+        larger = [keep.tile([P, PACK, HALF], BF16, name="larger0")]
+        z_g = [keep.tile([P, HALF * PACK], BF16, name="z_g%d" % h, align_bytes=64) for h in range(2)]
+
+        def fetch_y(t, h):
+            nc.vector.tensor_copy(fetched[h][:, t, :], y[t][:].indirect(half_list(n1_t, h)))
+
+        def take_max(t, h):
+            nc.vector.tensor_tensor(larger[h][:, t, :], y[t][:, cols(h)], fetched[h][:, t, :], ALU.max)
+
+        def weave(h):
+            nc.vector.tensor_copy(
+                out=z_g[h][:].rearrange("p (c i t) -> p c t i", i=8, t=PACK),
+                in_=larger[h][:].rearrange("p t (c i) -> p c t i", i=8),
+            )
+
+        for t in range(PACK):
+            fetch_y(t, 0)
+        for t in range(PACK):
+            fetch_y(t, 1)
+            take_max(t, 0)
+        weave(0)
+        w2_q = quantize("w2", w2_g[:], 512)
+        larger.append(keep.tile([P, PACK, HALF], BF16, name="w2_g", align_bytes=64))
+        take_max(0, 1)
+        take_max(1, 1)
+        z_q = [quantize("z0", z_g[0][:], HALF)]
+        take_max(2, 1)
+        take_max(3, 1)
+        w3_q = [quantize("w3a", w3_g[:, :1024], 256)]
+        weave(1)
+        w3_q.append(quantize("w3b", w3_g[:, 1024:], 256))
+
+        d = [keep.tile([P, S], F32, name="d%d" % t) for t in range(PACK)]
+        hs = [keep.tile([P, S], F32, name="h%d" % t) for t in range(PACK)]
+
+        def make_d(t):
+            acc = psum.tile([P, S], F32, name="bank%d" % (PACK + t))
+            product(acc[:], w3_q[t // 2], t % 2, b_words[:], b_bytes[:])
+            nc.scalar.copy(d[t][:], acc[:])
+
+        def make_h(h, pair):
+            acc = psum.tile([P, 2, HALF], F32, name="bank%d" % (2 * h + pair))
+            for u in range(2):
+                product(acc[:, u, :], w2_q, 2 * pair + u, z_q[h][0][:], z_q[h][1][:])
+            for u in range(2):
+                nc.scalar.activation(hs[2 * pair + u][:, cols(h)], acc[:, u, :], COPY, scale=0.75)
+
+        make_h(0, 0)
+        make_d(0)
+        make_d(1)
+        z_q.append(quantize("z1", z_g[1][:], HALF))
+        make_h(1, 0)
+        make_h(0, 1)
+        make_d(2)
+        make_h(1, 1)
+        make_d(3)
+
+        first = [keep.tile([P, S], F32, name="first%d" % t) for t in range(PACK)]
+        second = [keep.tile([P, S], F32, name="second%d" % t) for t in range(PACK)]
+        result = [keep.tile([P, S], F32, name="result%d" % t) for t in range(PACK)]
+        out_rows = out.rearrange("(b t i) n -> t b i n", t=PACK, i=8)
+
+        def first_term(t, h):
+            nc.vector.tensor_tensor(first[t][:, cols(h)], d[t][:].indirect(half_list(n3_t, h)), hs[t][:, cols(h)], ALU.mult)
+
+        def second_term(t, h):
+            nc.vector.tensor_tensor(second[t][:, cols(h)], hs[t][:].indirect(half_list(n2_t, h)), d[t][:, cols(h)], ALU.mult)
+
+        def finish(t, c):
+            nc.vector.tensor_tensor(result[t][:, c], first[t][:, c], second[t][:, c], ALU.subtract)
+            nc.sync.dma_start(out=out_rows[t][:, :, c], in_=result[t][:, c])
+
+        first_term(0, 0)
+        for t in range(PACK):
+            if t + 1 < PACK:
+                first_term(t + 1, 0)
+            second_term(t, 0)
+            if t > 0:
+                finish(t - 1, slice(0, S))
+            first_term(t, 1)
+            second_term(t, 1)
+        finish(PACK - 1, cols(0))
+        finish(PACK - 1, cols(1))

@@ -46,21 +46,25 @@ def tile_picked_latecrossbbig_none_p_kernel(
         def cols(h):
             return slice(h * HALF, (h + 1) * HALF)
 
-        x_bytes = keep.tile([P, T], U8, name="x_bytes", align_bytes=64)
-        nc.vector.memset(x_bytes[:].bitcast(I32), 0)
-        gain_block = keep.tile([P, 32], F32, name="gain_block")
-        nc.sync.dma_start(out=gain_block[:], in_=gn.rearrange("(b c) o -> b o c", c=32).to_broadcast([16, 8, 32]))
-        x_codes = keep.tile([P, T], U32, name="x_codes", align_bytes=64)
-        nc.sync.dma_start(out=x_codes[:].bitcast(I32), in_=x_words[0].rearrange("p n t -> p (n t)").bitcast(I32))
         offs_t = load_list("offs_t", offs)
         two_t = load_list("two_t", two)
+        gain_block = keep.tile([P, 32], F32, name="gain_block", align_bytes=64)
+        nc.sync.dma_start(out=gain_block[:], in_=gn.rearrange("(b c) o -> b o c", c=32).to_broadcast([16, 8, 32]))
+        x_bytes = keep.tile([P, T], U8, name="x_bytes", align_bytes=64)
+        scale_rows = x_scales[0].bitcast(I32)
+        for q in range(4):
+            nc.sync.dma_start(
+                out=x_bytes[32 * q : 32 * q + 32, :].bitcast(I32),
+                in_=scale_rows[4 * q : 4 * q + 4, :].unsqueeze(0).to_broadcast([8, 4, T // 4]),
+            )
+        x_codes = keep.tile([P, T], U32, name="x_codes", align_bytes=64)
+        nc.sync.dma_start(out=x_codes[:].bitcast(I32), in_=x_words[0].rearrange("p n t -> p (n t)").bitcast(I32))
+        w1_raw = [keep.tile([P, PACK, 256], F32, name="w1_raw%d" % h) for h in range(2)]
+        for h in range(2):
+            nc.sync.dma_start(out=w1_raw[h][:], in_=w1[:, 256 * h : 256 * (h + 1)].rearrange("(p j) c -> p j c", j=PACK))
         n1_t = load_list("n1_t", n1)
         n3_t = load_list("n3_t", n3)
         n2_t = load_list("n2_t", n2)
-        w1_raw = load_weight("w1_raw", w1)
-        scale_rows = x_scales[0].bitcast(I32)
-        for q in range(4):
-            nc.sync.dma_start(out=x_bytes[32 * q : 32 * q + 4, :].bitcast(I32), in_=scale_rows[4 * q : 4 * q + 4, :])
         w2_rows = w2.rearrange("(b j i) c -> j b i c", j=PACK, i=8)
         w2_raw = [keep.tile([P, 512], F32, name="w2_raw%d" % j) for j in range(PACK)]
         for j in range(PACK):
@@ -69,8 +73,11 @@ def tile_picked_latecrossbbig_none_p_kernel(
 
         ident = keep.tile([P, P], F32, name="ident")
         make_identity(nc, ident[:])
-        own = keep.tile([P, 8], F32, name="own")
-        nc.vector.tensor_reduce(own[:], ident[:].rearrange("p (b i) -> p i b", i=8), mybir.AxisListType.X, ALU.add)
+        own = ident
+        for width in (64, 32, 16, 8):
+            folded = keep.tile([P, width], F32, name="own%d" % width, align_bytes=64)
+            nc.gpsimd.tensor_tensor(folded[:], own[:, :width], own[:, width:], ALU.add)
+            own = folded
         picked = keep.tile([P, PACK, 8], F32, name="picked", align_bytes=64)
         nc.vector.tensor_tensor(
             picked[:], gain_block[:].rearrange("p (t i) -> p t i", i=8),
@@ -81,9 +88,9 @@ def tile_picked_latecrossbbig_none_p_kernel(
         mag = keep.tile([P, PACK], F32, name="mag")
         nc.vector.tensor_reduce(mag[:], picked[:], mybir.AxisListType.X, ALU.add, apply_absolute_value=True)
         nonneg = keep.tile([P, PACK], F32, name="nonneg", align_bytes=64)
-        nc.vector.tensor_scalar(nonneg[:], gain[:], 0.0, 2.0, ALU.is_ge, ALU.mult)
+        nc.gpsimd.tensor_scalar(nonneg[:], gain[:], 0.0, 2.0, ALU.is_ge, ALU.mult)
         sign = keep.tile([P, PACK], F32, name="sign")
-        nc.vector.tensor_scalar(sign[:], nonneg[:], 1.0, -1.0, ALU.mult, ALU.add)
+        nc.gpsimd.tensor_scalar(sign[:], nonneg[:], 1.0, -1.0, ALU.mult, ALU.add)
 
         def gather_bytes(name, lst):
             t = keep.tile([P, S], U8, name=name, align_bytes=64)
@@ -108,29 +115,32 @@ def tile_picked_latecrossbbig_none_p_kernel(
                 rhs=codes.bitcast(FP8X4), rhs_scale=scales, start=True, stop=True,
             )
 
-        def deal(dst, src, t):
-            nc.scalar.copy(
-                out=dst.rearrange("p (b i j) -> p b j i", i=8, j=PACK),
-                in_=src[:].rearrange("p j (b t i) -> p t b j i", t=PACK, i=8)[:, t],
+        def deal(copy, dst, src, t):
+            copy(
+                out=dst.rearrange("p (b u v j) -> p b u j v", u=2, v=4, j=PACK),
+                in_=src[:].rearrange("p j (b t u v) -> p t b u j v", t=PACK, u=2, v=4)[:, t],
             )
 
-        a_words = gather_words("nonneg", offs_t)
-        b_words = gather_words("picked", two_t)
-        a_bytes = gather_bytes("a_bytes", offs_t)
-        w1_q = []
-        for t in range(PACK):
-            w1_g = keep.tile([P, 512], BF16, name="w1_g%d" % t, align_bytes=64)
-            deal(w1_g[:], w1_raw, t)
-            w1_q.append(quantize("w1_%d" % t, w1_g[:], P))
-            if t == 1:
-                b_bytes = gather_bytes("w1_g1", two_t)
+        a_bytes = gather_bytes("picked", offs_t)
+        b_bytes = gather_bytes("own8", two_t)
+        words = keep.tile([P, 2 * S], U32, name="x_bytes", align_bytes=64)
+        a_words, b_words = words[:, :S], words[:, S:]
+        nc.vector.tensor_copy(a_words, x_codes[:].indirect(offs_t[:]))
+        nc.vector.tensor_copy(b_words, x_codes[:].indirect(two_t[:]))
+        w1_g = [keep.tile([P, 512], BF16, name="w1_g%d" % t, align_bytes=64) for t in range(PACK)]
+        for h in range(2):
+            for t in range(PACK):
+                deal(nc.scalar.copy, w1_g[t][:, 256 * h : 256 * (h + 1)], w1_raw[h], t)
+        w1_q = [quantize("w1_%d" % t, w1_g[t][:], P) for t in range(PACK)]
 
         y = []
         for t in range(PACK):
-            acc = psum.tile([P, S], F32, name="bank%d" % t)
-            product(acc[:], w1_q[t], 0, a_words[:], a_bytes[:])
             y_t = keep.tile([P, S], F32, name="y%d" % t)
-            nc.scalar.activation(y_t[:], acc[:], COPY, scale=mag[:, t : t + 1])
+            pieces = [(0, cols(0)), (PACK, cols(1))] if t == 0 else [(t, slice(0, S))]
+            for bank, c in pieces:
+                acc = psum.tile([P, S], F32, name="bank%d" % bank)
+                product(acc[:, c], w1_q[t], 0, a_words[:, c], a_bytes[:, c])
+                nc.scalar.activation(y_t[:, c], acc[:, c], COPY, scale=mag[:, t : t + 1])
             y.append(y_t)
 
         w2_signed = keep.tile([P, PACK, 512], BF16, name="mag")
@@ -140,9 +150,9 @@ def tile_picked_latecrossbbig_none_p_kernel(
         w2_g = keep.tile([P, 512 * PACK], BF16, name="w2_g", align_bytes=64)
         w3_g = keep.tile([P, 512 * PACK], BF16, name="w3_g", align_bytes=64)
         for t in range(PACK):
-            deal(w2_g[:, 512 * t : 512 * (t + 1)], w2_signed, t)
+            deal(nc.scalar.copy, w2_g[:, 512 * t : 512 * (t + 1)], w2_signed, t)
         for t in range(PACK):
-            deal(w3_g[:, 512 * t : 512 * (t + 1)], w3_raw, t)
+            deal(nc.scalar.copy, w3_g[:, 512 * t : 512 * (t + 1)], w3_raw, t)
 
         fetched = [keep.tile([P, PACK, HALF], F32, name="fetched%d" % h) for h in range(2)]
         larger = [keep.tile([P, PACK, HALF], BF16, name="larger0")]
@@ -156,8 +166,8 @@ def tile_picked_latecrossbbig_none_p_kernel(
 
         def weave(h):
             nc.vector.tensor_copy(
-                out=z_g[h][:].rearrange("p (c i t) -> p c t i", i=8, t=PACK),
-                in_=larger[h][:].rearrange("p t (c i) -> p c t i", i=8),
+                out=z_g[h][:].rearrange("p (c i t) -> p c t i", i=4, t=PACK),
+                in_=larger[h][:].rearrange("p t (c i) -> p c t i", i=4),
             )
 
         for t in range(PACK):
@@ -182,7 +192,7 @@ def tile_picked_latecrossbbig_none_p_kernel(
 
         def make_d(t):
             acc = psum.tile([P, S], F32, name="bank%d" % (PACK + t))
-            product(acc[:], w3_q[t // 2], t % 2, b_words[:], b_bytes[:])
+            product(acc[:], w3_q[t // 2], t % 2, b_words, b_bytes[:])
             nc.scalar.copy(d[t][:], acc[:])
 
         def make_h(h, pair):
@@ -210,21 +220,28 @@ def tile_picked_latecrossbbig_none_p_kernel(
         def first_term(t, h):
             nc.vector.tensor_tensor(first[t][:, cols(h)], d[t][:].indirect(half_list(n3_t, h)), hs[t][:, cols(h)], ALU.mult)
 
-        def second_term(t, h):
-            nc.vector.tensor_tensor(second[t][:, cols(h)], hs[t][:].indirect(half_list(n2_t, h)), d[t][:, cols(h)], ALU.mult)
+        def second_term(t, c):
+            entries = n2_t[:, c.start // 16 : c.stop // 16]
+            nc.vector.tensor_tensor(second[t][:, c], hs[t][:].indirect(entries), d[t][:, c], ALU.mult)
 
-        def finish(t, c):
+        def finish(t, c, queue=nc.sync):
             nc.vector.tensor_tensor(result[t][:, c], first[t][:, c], second[t][:, c], ALU.subtract)
-            nc.sync.dma_start(out=out_rows[t][:, :, c], in_=result[t][:, c])
+            queue.dma_start(out=out_rows[t][:, :, c], in_=result[t][:, c])
 
         first_term(0, 0)
-        for t in range(PACK):
-            if t + 1 < PACK:
-                first_term(t + 1, 0)
-            second_term(t, 0)
+        for t in range(PACK - 1):
+            first_term(t + 1, 0)
+            second_term(t, cols(0))
             if t > 0:
                 finish(t - 1, slice(0, S))
             first_term(t, 1)
-            second_term(t, 1)
-        finish(PACK - 1, cols(0))
-        finish(PACK - 1, cols(1))
+            second_term(t, cols(1))
+        last = PACK - 1
+        second_term(last, cols(0))
+        finish(last - 1, slice(0, S))
+        first_term(last, 1)
+        finish(last, cols(0))
+        second_term(last, slice(256, 384))
+        second_term(last, slice(384, 512))
+        finish(last, slice(256, 384), nc.scalar)
+        finish(last, slice(384, 512))

@@ -20,6 +20,7 @@ P = 128
 PACK = 4
 HALF = S // 2
 LIST_COLS = S // 16
+SUMMED_ON_PE = 2
 
 
 def tile_picked_latecrossbbig_none_p_kernel(
@@ -46,17 +47,16 @@ def tile_picked_latecrossbbig_none_p_kernel(
         def cols(h):
             return slice(h * HALF, (h + 1) * HALF)
 
-        offs_t = load_list("offs_t", offs)
-        two_t = load_list("two_t", two)
         gain_block = keep.tile([P, 32], F32, name="gain_block", align_bytes=64)
         nc.sync.dma_start(out=gain_block[:], in_=gn.rearrange("(b c) o -> b o c", c=32).to_broadcast([16, 8, 32]))
+        offs_t = load_list("offs_t", offs)
+        two_t = load_list("two_t", two)
+        x_rows = keep.tile([P, T // 4], I32, name="x_rows")
         x_bytes = keep.tile([P, T], U8, name="x_bytes", align_bytes=64)
+        nc.vector.memset(x_bytes[:].bitcast(I32), 0)
         scale_rows = x_scales[0].bitcast(I32)
         for q in range(4):
-            nc.sync.dma_start(
-                out=x_bytes[32 * q : 32 * q + 32, :].bitcast(I32),
-                in_=scale_rows[4 * q : 4 * q + 4, :].unsqueeze(0).to_broadcast([8, 4, T // 4]),
-            )
+            nc.sync.dma_start(out=x_rows[32 * q : 32 * q + 4, :], in_=scale_rows[4 * q : 4 * q + 4, :])
         x_codes = keep.tile([P, T], U32, name="x_codes", align_bytes=64)
         nc.sync.dma_start(out=x_codes[:].bitcast(I32), in_=x_words[0].rearrange("p n t -> p (n t)").bitcast(I32))
         w1_raw = [keep.tile([P, PACK, 256], F32, name="w1_raw%d" % h) for h in range(2)]
@@ -121,17 +121,18 @@ def tile_picked_latecrossbbig_none_p_kernel(
                 in_=src[:].rearrange("p j (b t u v) -> p t b u j v", t=PACK, u=2, v=4)[:, t],
             )
 
+        for q in range(4):
+            nc.vector.tensor_copy(x_bytes[32 * q : 32 * q + 4, :].bitcast(I32), x_rows[32 * q : 32 * q + 4, :])
         a_bytes = gather_bytes("picked", offs_t)
         b_bytes = gather_bytes("own8", two_t)
-        words = keep.tile([P, 2 * S], U32, name="x_bytes", align_bytes=64)
-        a_words, b_words = words[:, :S], words[:, S:]
-        nc.vector.tensor_copy(a_words, x_codes[:].indirect(offs_t[:]))
-        nc.vector.tensor_copy(b_words, x_codes[:].indirect(two_t[:]))
+        a_words = gather_words("x_bytes", offs_t)[:]
         w1_g = [keep.tile([P, 512], BF16, name="w1_g%d" % t, align_bytes=64) for t in range(PACK)]
         for h in range(2):
             for t in range(PACK):
                 deal(nc.scalar.copy, w1_g[t][:, 256 * h : 256 * (h + 1)], w1_raw[h], t)
-        w1_q = [quantize("w1_%d" % t, w1_g[t][:], P) for t in range(PACK)]
+        w1_q = [quantize("w1_0", w1_g[0][:], P)]
+        b_words = gather_words("w1_g0", two_t)[:]
+        w1_q.extend(quantize("w1_%d" % t, w1_g[t][:], P) for t in range(1, PACK))
 
         y = []
         for t in range(PACK):
@@ -143,19 +144,21 @@ def tile_picked_latecrossbbig_none_p_kernel(
                 nc.scalar.activation(y_t[:, c], acc[:, c], COPY, scale=mag[:, t : t + 1])
             y.append(y_t)
 
-        w2_signed = keep.tile([P, PACK, 512], BF16, name="mag")
+        w2_signed = keep.tile([P, PACK, 512], BF16, name="w2_signed")
         for j in range(PACK):
-            nc.scalar.activation(w2_signed[:, j, :], w2_raw[j][:], COPY, scale=sign[:, j : j + 1])
+            nc.gpsimd.tensor_scalar(w2_signed[:, j, :], w2_raw[j][:], sign[:, j : j + 1], 0.0, ALU.mult, ALU.add)
 
         w2_g = keep.tile([P, 512 * PACK], BF16, name="w2_g", align_bytes=64)
         w3_g = keep.tile([P, 512 * PACK], BF16, name="w3_g", align_bytes=64)
+        for t in range(2):
+            deal(nc.scalar.copy, w3_g[:, 512 * t : 512 * (t + 1)], w3_raw, t)
         for t in range(PACK):
             deal(nc.scalar.copy, w2_g[:, 512 * t : 512 * (t + 1)], w2_signed, t)
-        for t in range(PACK):
+        for t in range(2, PACK):
             deal(nc.scalar.copy, w3_g[:, 512 * t : 512 * (t + 1)], w3_raw, t)
 
         fetched = [keep.tile([P, PACK, HALF], F32, name="fetched%d" % h) for h in range(2)]
-        larger = [keep.tile([P, PACK, HALF], BF16, name="larger0")]
+        larger = [keep.tile([P, PACK, HALF], BF16, name="w2_raw3")]
         z_g = [keep.tile([P, HALF * PACK], BF16, name="z_g%d" % h, align_bytes=64) for h in range(2)]
 
         def fetch_y(t, h):
@@ -175,6 +178,7 @@ def tile_picked_latecrossbbig_none_p_kernel(
         for t in range(PACK):
             fetch_y(t, 1)
             take_max(t, 0)
+        w3_q = [quantize("w3a", w3_g[:, :1024], 256)]
         weave(0)
         w2_q = quantize("w2", w2_g[:], 512)
         larger.append(keep.tile([P, PACK, HALF], BF16, name="w2_g", align_bytes=64))
@@ -183,17 +187,19 @@ def tile_picked_latecrossbbig_none_p_kernel(
         z_q = [quantize("z0", z_g[0][:], HALF)]
         take_max(2, 1)
         take_max(3, 1)
-        w3_q = [quantize("w3a", w3_g[:, :1024], 256)]
-        weave(1)
         w3_q.append(quantize("w3b", w3_g[:, 1024:], 256))
+        weave(1)
 
         d = [keep.tile([P, S], F32, name="d%d" % t) for t in range(PACK)]
+        d_neg = [keep.tile([P, S], F32, name="d_neg%d" % t) for t in range(SUMMED_ON_PE)]
         hs = [keep.tile([P, S], F32, name="h%d" % t) for t in range(PACK)]
 
         def make_d(t):
             acc = psum.tile([P, S], F32, name="bank%d" % (PACK + t))
             product(acc[:], w3_q[t // 2], t % 2, b_words, b_bytes[:])
             nc.scalar.copy(d[t][:], acc[:])
+            if t < SUMMED_ON_PE:
+                nc.scalar.activation(d_neg[t][:], acc[:], COPY, scale=-1.0)
 
         def make_h(h, pair):
             acc = psum.tile([P, 2, HALF], F32, name="bank%d" % (2 * h + pair))
@@ -202,12 +208,12 @@ def tile_picked_latecrossbbig_none_p_kernel(
             for u in range(2):
                 nc.scalar.activation(hs[2 * pair + u][:, cols(h)], acc[:, u, :], COPY, scale=0.75)
 
-        make_h(0, 0)
         make_d(0)
         make_d(1)
+        make_h(0, 0)
         z_q.append(quantize("z1", z_g[1][:], HALF))
-        make_h(1, 0)
         make_h(0, 1)
+        make_h(1, 0)
         make_d(2)
         make_h(1, 1)
         make_d(3)
@@ -222,10 +228,24 @@ def tile_picked_latecrossbbig_none_p_kernel(
 
         def second_term(t, c):
             entries = n2_t[:, c.start // 16 : c.stop // 16]
-            nc.vector.tensor_tensor(second[t][:, c], hs[t][:].indirect(entries), d[t][:, c], ALU.mult)
+            nc.vector.tensor_tensor(second[t][:, c], hs[t][:].indirect(entries), (d_neg if t < SUMMED_ON_PE else d)[t][:, c], ALU.mult)
 
-        def finish(t, c, queue=nc.sync):
-            nc.vector.tensor_tensor(result[t][:, c], first[t][:, c], second[t][:, c], ALU.subtract)
+        def finish(t, c):
+            queue = nc.scalar if t < SUMMED_ON_PE else nc.sync
+            if t < SUMMED_ON_PE:
+                turned = psum.tile([P, PACK, P], F32, name="bank%d" % (PACK + t))
+                for k in range(PACK):
+                    block = slice(k * P, (k + 1) * P)
+                    nc.tensor.matmul(turned[:, k, :], first[t][:, block], ident[:], start=True, stop=False, is_transpose=True)
+                    nc.tensor.matmul(turned[:, k, :], second[t][:, block], ident[:], start=False, stop=True, is_transpose=True)
+                summed = keep.tile([P, PACK, P], F32, name="summed%d" % t)
+                nc.scalar.copy(summed[:], turned[:])
+                back = psum.tile([P, PACK, P], F32, name="bank%d" % t)
+                for k in range(PACK):
+                    nc.tensor.transpose(back[:, k, :], summed[:, k, :], ident[:])
+                nc.scalar.copy(result[t][:].rearrange("p (k c) -> p k c", k=PACK), back[:])
+            else:
+                nc.vector.tensor_tensor(result[t][:, c], first[t][:, c], second[t][:, c], ALU.subtract)
             queue.dma_start(out=out_rows[t][:, :, c], in_=result[t][:, c])
 
         first_term(0, 0)
@@ -243,5 +263,5 @@ def tile_picked_latecrossbbig_none_p_kernel(
         finish(last, cols(0))
         second_term(last, slice(256, 384))
         second_term(last, slice(384, 512))
-        finish(last, slice(256, 384), nc.scalar)
+        finish(last, slice(256, 384))
         finish(last, slice(384, 512))

@@ -20,7 +20,7 @@ P = 128
 PACK = 4
 HALF = S // 2
 LIST_COLS = S // 16
-SUMMED_ON_PE = 2
+SUMMED_ON_PE = 3
 
 
 def tile_picked_latecrossbbig_none_p_kernel(
@@ -47,16 +47,16 @@ def tile_picked_latecrossbbig_none_p_kernel(
         def cols(h):
             return slice(h * HALF, (h + 1) * HALF)
 
-        gain_block = keep.tile([P, 32], F32, name="gain_block", align_bytes=64)
-        nc.sync.dma_start(out=gain_block[:], in_=gn.rearrange("(b c) o -> b o c", c=32).to_broadcast([16, 8, 32]))
-        offs_t = load_list("offs_t", offs)
-        two_t = load_list("two_t", two)
         x_rows = keep.tile([P, T // 4], I32, name="x_rows")
         x_bytes = keep.tile([P, T], U8, name="x_bytes", align_bytes=64)
         nc.vector.memset(x_bytes[:].bitcast(I32), 0)
         scale_rows = x_scales[0].bitcast(I32)
         for q in range(4):
             nc.sync.dma_start(out=x_rows[32 * q : 32 * q + 4, :], in_=scale_rows[4 * q : 4 * q + 4, :])
+        gain_block = keep.tile([P, 32], F32, name="gain_block", align_bytes=64)
+        nc.sync.dma_start(out=gain_block[:], in_=gn.rearrange("(b c) o -> b o c", c=32).to_broadcast([16, 8, 32]))
+        offs_t = load_list("offs_t", offs)
+        two_t = load_list("two_t", two)
         x_codes = keep.tile([P, T], U32, name="x_codes", align_bytes=64)
         nc.sync.dma_start(out=x_codes[:].bitcast(I32), in_=x_words[0].rearrange("p n t -> p (n t)").bitcast(I32))
         w1_raw = [keep.tile([P, PACK, 256], F32, name="w1_raw%d" % h) for h in range(2)]
@@ -157,15 +157,18 @@ def tile_picked_latecrossbbig_none_p_kernel(
         for t in range(2, PACK):
             deal(nc.scalar.copy, w3_g[:, 512 * t : 512 * (t + 1)], w3_raw, t)
 
-        fetched = [keep.tile([P, PACK, HALF], F32, name="fetched%d" % h) for h in range(2)]
-        larger = [keep.tile([P, PACK, HALF], BF16, name="w2_raw3")]
+        y_rounded = keep.tile([P, PACK, S], BF16, name="y_rounded")
+        for t in range(PACK):
+            nc.gpsimd.tensor_scalar(y_rounded[:, t, :], y[t][:], 1.0, 0.0, ALU.mult, ALU.add)
+        fetched = [keep.tile([P, PACK, HALF], BF16, name="fetched%d" % h) for h in range(2)]
+        larger = [keep.tile([P, PACK, HALF], BF16, name="larger0")]
         z_g = [keep.tile([P, HALF * PACK], BF16, name="z_g%d" % h, align_bytes=64) for h in range(2)]
 
         def fetch_y(t, h):
             nc.vector.tensor_copy(fetched[h][:, t, :], y[t][:].indirect(half_list(n1_t, h)))
 
-        def take_max(t, h):
-            nc.vector.tensor_tensor(larger[h][:, t, :], y[t][:, cols(h)], fetched[h][:, t, :], ALU.max)
+        def take_max(h):
+            nc.vector.tensor_tensor(larger[h][:], y_rounded[:, :, cols(h)], fetched[h][:], ALU.max)
 
         def weave(h):
             nc.vector.tensor_copy(
@@ -177,16 +180,13 @@ def tile_picked_latecrossbbig_none_p_kernel(
             fetch_y(t, 0)
         for t in range(PACK):
             fetch_y(t, 1)
-            take_max(t, 0)
+        take_max(0)
         w3_q = [quantize("w3a", w3_g[:, :1024], 256)]
         weave(0)
         w2_q = quantize("w2", w2_g[:], 512)
         larger.append(keep.tile([P, PACK, HALF], BF16, name="w2_g", align_bytes=64))
-        take_max(0, 1)
-        take_max(1, 1)
+        take_max(1)
         z_q = [quantize("z0", z_g[0][:], HALF)]
-        take_max(2, 1)
-        take_max(3, 1)
         w3_q.append(quantize("w3b", w3_g[:, 1024:], 256))
         weave(1)
 
@@ -212,8 +212,8 @@ def tile_picked_latecrossbbig_none_p_kernel(
         make_d(1)
         make_h(0, 0)
         z_q.append(quantize("z1", z_g[1][:], HALF))
-        make_h(0, 1)
         make_h(1, 0)
+        make_h(0, 1)
         make_d(2)
         make_h(1, 1)
         make_d(3)
@@ -230,38 +230,37 @@ def tile_picked_latecrossbbig_none_p_kernel(
             entries = n2_t[:, c.start // 16 : c.stop // 16]
             nc.vector.tensor_tensor(second[t][:, c], hs[t][:].indirect(entries), (d_neg if t < SUMMED_ON_PE else d)[t][:, c], ALU.mult)
 
-        def finish(t, c):
-            queue = nc.scalar if t < SUMMED_ON_PE else nc.sync
-            if t < SUMMED_ON_PE:
-                turned = psum.tile([P, PACK, P], F32, name="bank%d" % (PACK + t))
-                for k in range(PACK):
-                    block = slice(k * P, (k + 1) * P)
-                    nc.tensor.matmul(turned[:, k, :], first[t][:, block], ident[:], start=True, stop=False, is_transpose=True)
-                    nc.tensor.matmul(turned[:, k, :], second[t][:, block], ident[:], start=False, stop=True, is_transpose=True)
-                summed = keep.tile([P, PACK, P], F32, name="summed%d" % t)
-                nc.scalar.copy(summed[:], turned[:])
-                back = psum.tile([P, PACK, P], F32, name="bank%d" % t)
-                for k in range(PACK):
-                    nc.tensor.transpose(back[:, k, :], summed[:, k, :], ident[:])
-                nc.scalar.copy(result[t][:].rearrange("p (k c) -> p k c", k=PACK), back[:])
-            else:
-                nc.vector.tensor_tensor(result[t][:, c], first[t][:, c], second[t][:, c], ALU.subtract)
-            queue.dma_start(out=out_rows[t][:, :, c], in_=result[t][:, c])
+        def finish_on_tensor(t, h):
+            turned = psum.tile([P, 2, P], F32, name="bank%d" % (PACK + h))
+            for k in range(2):
+                block = slice(h * HALF + k * P, h * HALF + (k + 1) * P)
+                nc.tensor.matmul(turned[:, k, :], first[t][:, block], ident[:], start=True, stop=False, is_transpose=True)
+                nc.tensor.matmul(turned[:, k, :], second[t][:, block], ident[:], start=False, stop=True, is_transpose=True)
+            summed = keep.tile([P, 2, P], F32, name="summed%d" % h)
+            nc.scalar.copy(summed[:], turned[:])
+            back = psum.tile([P, 2, P], F32, name="bank%d" % h)
+            for k in range(2):
+                nc.tensor.transpose(back[:, k, :], summed[:, k, :], ident[:])
+            nc.scalar.copy(result[t][:, cols(h)].rearrange("p (k c) -> p k c", k=2), back[:])
+            nc.scalar.dma_start(out=out_rows[t][:, :, cols(h)], in_=result[t][:, cols(h)])
+
+        def finish_on_vector(t, c):
+            nc.vector.tensor_tensor(result[t][:, c], first[t][:, c], second[t][:, c], ALU.subtract)
+            nc.sync.dma_start(out=out_rows[t][:, :, c], in_=result[t][:, c])
 
         first_term(0, 0)
-        for t in range(PACK - 1):
+        for t in range(SUMMED_ON_PE):
             first_term(t + 1, 0)
             second_term(t, cols(0))
-            if t > 0:
-                finish(t - 1, slice(0, S))
+            finish_on_tensor(t, 0)
             first_term(t, 1)
             second_term(t, cols(1))
+            finish_on_tensor(t, 1)
         last = PACK - 1
         second_term(last, cols(0))
-        finish(last - 1, slice(0, S))
         first_term(last, 1)
-        finish(last, cols(0))
+        finish_on_vector(last, cols(0))
         second_term(last, slice(256, 384))
         second_term(last, slice(384, 512))
-        finish(last, slice(256, 384))
-        finish(last, slice(384, 512))
+        finish_on_vector(last, slice(256, 384))
+        finish_on_vector(last, slice(384, 512))

@@ -20,7 +20,7 @@ P = 128
 PACK = 4
 HALF = S // 2
 LIST_COLS = S // 16
-SUMMED_ON_PE = 3
+SUMMED_ON_PE = 2
 
 
 def tile_picked_latecrossbbig_none_p_kernel(
@@ -249,14 +249,20 @@ def tile_picked_latecrossbbig_none_p_kernel(
             nc.sync.dma_start(out=out_rows[t][:, :, c], in_=result[t][:, c])
 
         first_term(0, 0)
+        first_term(1, 0)
         for t in range(SUMMED_ON_PE):
-            first_term(t + 1, 0)
             second_term(t, cols(0))
             finish_on_tensor(t, 0)
             first_term(t, 1)
             second_term(t, cols(1))
             finish_on_tensor(t, 1)
+        first_term(2, 0)
+        second_term(2, cols(0))
+        first_term(2, 1)
+        second_term(2, cols(1))
         last = PACK - 1
+        first_term(last, 0)
+        finish_on_vector(2, slice(0, S))
         second_term(last, cols(0))
         first_term(last, 1)
         finish_on_vector(last, cols(0))

from contextlib import ExitStack

import concourse.mybir as mybir
from concourse.masks import make_identity

K, T, S, N, H = 512, 2048, 512, 512, 512
FLOPS = 3 * 2 * 512 * 512 * 512

F32 = mybir.dt.float32
BF16 = mybir.dt.bfloat16
I32 = mybir.dt.int32
U32 = mybir.dt.uint32
U16 = mybir.dt.uint16
U8 = mybir.dt.uint8
FP8X4 = mybir.dt.float8_e4m3fn_x4
ALU = mybir.AluOpType
COPY = mybir.ActivationFunctionType.Copy

P = 128
PACK = 4
HALF = S // 2
LIST_COLS = S // 16
SUMMED_ON_PE = 2


def tile_picked_latecrossbbig_none_p_kernel(
    tc, x_words, x_scales, w1, gn, w2, w3, offs, n1, two, n2, n3, out
):
    nc = tc.nc
    with ExitStack() as ctx:
        keep = ctx.enter_context(tc.tile_pool(name="keep", bufs=1))
        psum = ctx.enter_context(tc.psum_pool(name="psum", bufs=1))

        def load_list(name, src):
            t = keep.tile([P, LIST_COLS], U16, name=name)
            nc.sync.dma_start(t[:], src)
            return t

        def load_weight(name, src):
            t = keep.tile([P, PACK, 512], F32, name=name)
            nc.sync.dma_start(out=t[:], in_=src.rearrange("(p j) c -> p j c", j=PACK))
            return t

        def half_list(t, h):
            return t[:, h * (LIST_COLS // 2) : (h + 1) * (LIST_COLS // 2)]

        def cols(h):
            return slice(h * HALF, (h + 1) * HALF)

        x_rows = keep.tile([P, T // 4], I32, name="x_rows")
        x_bytes = keep.tile([P, T], U8, name="x_bytes", align_bytes=64)
        nc.vector.memset(x_bytes[:].bitcast(I32), 0)
        scale_rows = x_scales[0].bitcast(I32)
        for q in range(4):
            nc.sync.dma_start(out=x_rows[32 * q : 32 * q + 4, :], in_=scale_rows[4 * q : 4 * q + 4, :])
        gain_block = keep.tile([P, 32], F32, name="gain_block", align_bytes=64)
        nc.sync.dma_start(out=gain_block[:], in_=gn.rearrange("(b c) o -> b o c", c=32).to_broadcast([16, 8, 32]))
        offs_t = load_list("offs_t", offs)
        two_t = load_list("two_t", two)
        x_codes = keep.tile([P, T], U32, name="x_codes", align_bytes=64)
        nc.sync.dma_start(out=x_codes[:].bitcast(I32), in_=x_words[0].rearrange("p n t -> p (n t)").bitcast(I32))
        w1_raw = [keep.tile([P, PACK, 256], F32, name="w1_raw%d" % h) for h in range(2)]
        for h in range(2):
            nc.sync.dma_start(out=w1_raw[h][:], in_=w1[:, 256 * h : 256 * (h + 1)].rearrange("(p j) c -> p j c", j=PACK))
        n1_t = load_list("n1_t", n1)
        n3_t = load_list("n3_t", n3)
        n2_t = load_list("n2_t", n2)
        w2_rows = w2.rearrange("(b j i) c -> j b i c", j=PACK, i=8)
        w2_raw = [keep.tile([P, 512], F32, name="w2_raw%d" % j) for j in range(PACK)]
        for j in range(PACK):
            nc.sync.dma_start(out=w2_raw[j][:], in_=w2_rows[j])
        w3_raw = load_weight("w3_raw", w3)

        ident = keep.tile([P, P], F32, name="ident")
        make_identity(nc, ident[:])
        own = ident
        for width in (64, 32, 16, 8):
            folded = keep.tile([P, width], F32, name="own%d" % width, align_bytes=64)
            nc.gpsimd.tensor_tensor(folded[:], own[:, :width], own[:, width:], ALU.add)
            own = folded
        picked = keep.tile([P, PACK, 8], F32, name="picked", align_bytes=64)
        nc.vector.tensor_tensor(
            picked[:], gain_block[:].rearrange("p (t i) -> p t i", i=8),
            own[:].unsqueeze(1).to_broadcast([P, PACK, 8]), ALU.mult,
        )
        gain = keep.tile([P, PACK], F32, name="gain")
        nc.vector.tensor_reduce(gain[:], picked[:], mybir.AxisListType.X, ALU.add)
        mag = keep.tile([P, PACK], F32, name="mag")
        nc.vector.tensor_reduce(mag[:], picked[:], mybir.AxisListType.X, ALU.add, apply_absolute_value=True)
        nonneg = keep.tile([P, PACK], F32, name="nonneg", align_bytes=64)
        nc.gpsimd.tensor_scalar(nonneg[:], gain[:], 0.0, 2.0, ALU.is_ge, ALU.mult)
        sign = keep.tile([P, PACK], F32, name="sign")
        nc.gpsimd.tensor_scalar(sign[:], nonneg[:], 1.0, -1.0, ALU.mult, ALU.add)

        def gather_bytes(name, lst):
            t = keep.tile([P, S], U8, name=name, align_bytes=64)
            nc.vector.tensor_copy(t[:], x_bytes[:].indirect(lst[:]))
            return t

        def gather_words(name, lst):
            t = keep.tile([P, S], U32, name=name, align_bytes=64)
            nc.vector.tensor_copy(t[:], x_codes[:].indirect(lst[:]))
            return t

        def quantize(name, grouped, width):
            codes = keep.tile([P, width], U32, name=name + "_codes", align_bytes=64)
            scales = keep.tile([P, width], U8, name=name + "_scales", align_bytes=64)
            nc.vector.quantize_mx(out=codes[:].bitcast(FP8X4), scales=scales[:], in_=grouped)
            return codes, scales

        def product(acc, w_q, t, codes, scales):
            m = slice(t * P, (t + 1) * P)
            nc.tensor.matmul_mx(
                out=acc, lhsT=w_q[0][:, m].bitcast(FP8X4), lhsT_scale=w_q[1][:, m],
                rhs=codes.bitcast(FP8X4), rhs_scale=scales, start=True, stop=True,
            )

        def deal(copy, dst, src, t):
            copy(
                out=dst.rearrange("p (b u v j) -> p b u j v", u=2, v=4, j=PACK),
                in_=src[:].rearrange("p j (b t u v) -> p t b u j v", t=PACK, u=2, v=4)[:, t],
            )

        for q in range(4):
            nc.vector.tensor_copy(x_bytes[32 * q : 32 * q + 4, :].bitcast(I32), x_rows[32 * q : 32 * q + 4, :])
        a_bytes = gather_bytes("picked", offs_t)
        b_bytes = gather_bytes("own8", two_t)
        a_words = gather_words("x_bytes", offs_t)[:]
        w1_g = [keep.tile([P, 512], BF16, name="w1_g%d" % t, align_bytes=64) for t in range(PACK)]
        for h in range(2):
            for t in range(PACK):
                deal(nc.scalar.copy, w1_g[t][:, 256 * h : 256 * (h + 1)], w1_raw[h], t)
        w1_q = [quantize("w1_0", w1_g[0][:], P)]
        b_words = gather_words("w1_g0", two_t)[:]
        w1_q.extend(quantize("w1_%d" % t, w1_g[t][:], P) for t in range(1, PACK))

        y = []
        for t in range(PACK):
            y_t = keep.tile([P, S], F32, name="y%d" % t)
            pieces = [(0, cols(0)), (PACK, cols(1))] if t == 0 else [(t, slice(0, S))]
            for bank, c in pieces:
                acc = psum.tile([P, S], F32, name="bank%d" % bank)
                product(acc[:, c], w1_q[t], 0, a_words[:, c], a_bytes[:, c])
                nc.scalar.activation(y_t[:, c], acc[:, c], COPY, scale=mag[:, t : t + 1])
            y.append(y_t)

        w2_signed = keep.tile([P, PACK, 512], BF16, name="w2_signed")
        for j in range(PACK):
            nc.gpsimd.tensor_scalar(w2_signed[:, j, :], w2_raw[j][:], sign[:, j : j + 1], 0.0, ALU.mult, ALU.add)

        w2_g = keep.tile([P, 512 * PACK], BF16, name="w2_g", align_bytes=64)
        w3_g = keep.tile([P, 512 * PACK], BF16, name="w3_g", align_bytes=64)
        for t in range(2):
            deal(nc.scalar.copy, w3_g[:, 512 * t : 512 * (t + 1)], w3_raw, t)
        for t in range(PACK):
            deal(nc.scalar.copy, w2_g[:, 512 * t : 512 * (t + 1)], w2_signed, t)
        for t in range(2, PACK):
            deal(nc.scalar.copy, w3_g[:, 512 * t : 512 * (t + 1)], w3_raw, t)

        y_rounded = keep.tile([P, PACK, S], BF16, name="y_rounded")
        for t in range(PACK):
            nc.gpsimd.tensor_scalar(y_rounded[:, t, :], y[t][:], 1.0, 0.0, ALU.mult, ALU.add)
        fetched = [keep.tile([P, PACK, HALF], BF16, name="fetched%d" % h) for h in range(2)]
        larger = [keep.tile([P, PACK, HALF], BF16, name="larger0")]
        z_g = [keep.tile([P, HALF * PACK], BF16, name="z_g%d" % h, align_bytes=64) for h in range(2)]

        def fetch_y(t, h):
            nc.vector.tensor_copy(fetched[h][:, t, :], y[t][:].indirect(half_list(n1_t, h)))

        def take_max(h):
            nc.vector.tensor_tensor(larger[h][:], y_rounded[:, :, cols(h)], fetched[h][:], ALU.max)

        def weave(h):
            nc.vector.tensor_copy(
                out=z_g[h][:].rearrange("p (c i t) -> p c t i", i=4, t=PACK),
                in_=larger[h][:].rearrange("p t (c i) -> p c t i", i=4),
            )

        for t in range(PACK):
            fetch_y(t, 0)
        for t in range(PACK):
            fetch_y(t, 1)
        take_max(0)
        w3_q = [quantize("w3a", w3_g[:, :1024], 256)]
        weave(0)
        w2_q = quantize("w2", w2_g[:], 512)
        larger.append(keep.tile([P, PACK, HALF], BF16, name="w2_g", align_bytes=64))
        take_max(1)
        z_q = [quantize("z0", z_g[0][:], HALF)]
        w3_q.append(quantize("w3b", w3_g[:, 1024:], 256))
        weave(1)

        d = [keep.tile([P, S], F32, name="d%d" % t) for t in range(PACK)]
        d_neg = [keep.tile([P, S], F32, name="d_neg%d" % t) for t in range(SUMMED_ON_PE)]
        hs = [keep.tile([P, S], F32, name="h%d" % t) for t in range(PACK)]

        def make_d(t):
            acc = psum.tile([P, S], F32, name="bank%d" % (PACK + t))
            product(acc[:], w3_q[t // 2], t % 2, b_words, b_bytes[:])
            nc.scalar.copy(d[t][:], acc[:])
            if t < SUMMED_ON_PE:
                nc.scalar.activation(d_neg[t][:], acc[:], COPY, scale=-1.0)

        def make_h(h, pair):
            acc = psum.tile([P, 2, HALF], F32, name="bank%d" % (2 * h + pair))
            for u in range(2):
                product(acc[:, u, :], w2_q, 2 * pair + u, z_q[h][0][:], z_q[h][1][:])
            for u in range(2):
                nc.scalar.activation(hs[2 * pair + u][:, cols(h)], acc[:, u, :], COPY, scale=0.75)

        make_d(0)
        make_d(1)
        make_h(0, 0)
        z_q.append(quantize("z1", z_g[1][:], HALF))
        make_h(1, 0)
        make_h(0, 1)
        make_d(2)
        make_h(1, 1)
        make_d(3)

        first = [keep.tile([P, S], F32, name="first%d" % t) for t in range(PACK)]
        second = [keep.tile([P, S], F32, name="second%d" % t) for t in range(PACK)]
        result = [keep.tile([P, S], F32, name="result%d" % t) for t in range(PACK)]
        out_rows = out.rearrange("(b t i) n -> t b i n", t=PACK, i=8)

        def first_term(t, h):
            nc.vector.tensor_tensor(first[t][:, cols(h)], d[t][:].indirect(half_list(n3_t, h)), hs[t][:, cols(h)], ALU.mult)

        def second_term(t, c):
            entries = n2_t[:, c.start // 16 : c.stop // 16]
            nc.vector.tensor_tensor(second[t][:, c], hs[t][:].indirect(entries), (d_neg if t < SUMMED_ON_PE else d)[t][:, c], ALU.mult)

        def finish_on_tensor(t, h):
            turned = psum.tile([P, 2, P], F32, name="bank%d" % (PACK + h))
            for k in range(2):
                block = slice(h * HALF + k * P, h * HALF + (k + 1) * P)
                nc.tensor.matmul(turned[:, k, :], first[t][:, block], ident[:], start=True, stop=False, is_transpose=True)
                nc.tensor.matmul(turned[:, k, :], second[t][:, block], ident[:], start=False, stop=True, is_transpose=True)
            summed = keep.tile([P, 2, P], F32, name="summed%d" % h)
            nc.scalar.copy(summed[:], turned[:])
            back = psum.tile([P, 2, P], F32, name="bank%d" % h)
            for k in range(2):
                nc.tensor.transpose(back[:, k, :], summed[:, k, :], ident[:])
            nc.scalar.copy(result[t][:, cols(h)].rearrange("p (k c) -> p k c", k=2), back[:])
            nc.scalar.dma_start(out=out_rows[t][:, :, cols(h)], in_=result[t][:, cols(h)])

        def finish_on_vector(t, c):
            nc.vector.tensor_tensor(result[t][:, c], first[t][:, c], second[t][:, c], ALU.subtract)
            nc.sync.dma_start(out=out_rows[t][:, :, c], in_=result[t][:, c])

        first_term(0, 0)
        first_term(1, 0)
        for t in range(SUMMED_ON_PE):
            second_term(t, cols(0))
            finish_on_tensor(t, 0)
            first_term(t, 1)
            second_term(t, cols(1))
            finish_on_tensor(t, 1)
        first_term(2, 0)
        second_term(2, cols(0))
        first_term(2, 1)
        second_term(2, cols(1))
        last = PACK - 1
        first_term(last, 0)
        finish_on_vector(2, slice(0, S))
        second_term(last, cols(0))
        first_term(last, 1)
        finish_on_vector(last, cols(0))
        second_term(last, slice(256, 384))
        second_term(last, slice(384, 512))
        finish_on_vector(last, slice(256, 384))
        finish_on_vector(last, slice(384, 512))
